import numpy as np
import ml_dtypes


def mxq(x, axis, fmt="e4m3"):
    dtype, down = {"e4m3": (ml_dtypes.float8_e4m3fn, 7), "e5m2": (ml_dtypes.float8_e5m2, 14)}[fmt]
    v = np.moveaxis(np.asarray(x, np.float32).astype(ml_dtypes.bfloat16).astype(np.float64), axis, -1)
    blocks = v.reshape(v.shape[:-1] + (-1, 32))
    amax = np.abs(blocks).max(-1, keepdims=True)
    byte = np.maximum(np.where(amax > 0, np.frexp(amax)[1] - 1 + 127, 0) - down, 1)
    scale = np.exp2(byte - 127.0)
    codes = (blocks / scale).astype(np.float32).astype(dtype).astype(np.float64)
    return np.moveaxis((codes * scale).reshape(v.shape), -1, axis)


WIDE = False


def mx_kscale(k):
    if not WIDE:
        return np.ones(k)
    levels = np.array([10, -10, 5, -5, 0])
    if k % 512:
        return np.exp2(np.random.permutation(np.resize(levels, k // 32))).repeat(32)
    a = np.empty((k // 512, 16))
    for p in range(k // 512):
        a[p, :8] = np.random.permutation(np.resize(levels, 8))
        for g in range(8):
            far = levels[np.abs(levels - a[p, g]) >= 10]
            a[p, g + 8] = far[np.random.randint(len(far))]
    return np.exp2(a.ravel()).repeat(32)


def f64(x):
    return np.asarray(x).astype(np.float64)


def striped(idx):
    return np.tile(idx.reshape(-1, 16).T, (8, 1)).astype(np.uint16)


def unstriped(offs):
    return offs[:16].T.reshape(-1).astype(np.int64)


E2M1 = np.array([0.0, 0.5, 1.0, 1.5, 2.0, 3.0, 4.0, 6.0, -0.0, -0.5, -1.0, -1.5, -2.0, -3.0, -4.0, -6.0])


def pack_weight(w, fmt):
    k, n = w.shape
    w = f64(np.asarray(w, np.float32).astype(ml_dtypes.bfloat16)).reshape(k // 32, 32, n)
    amax = np.abs(w).max(1)
    if fmt == "e4m3":
        byte = np.frexp(amax)[1] - 1 + 127 - 7
    else:
        mant, ex = np.frexp(amax / 6.0)
        byte = np.where(mant > 0.5, ex, ex - 1) + 127
    byte = np.clip(np.where(amax > 0, byte, 1), 1, 254)
    scaled = (w * np.exp2(127.0 - byte)[:, None, :]).reshape(k, n).astype(np.float32)
    by_word = np.ascontiguousarray(scaled.reshape(k // 512, 128, 4, n).transpose(0, 1, 3, 2))
    if fmt == "e4m3":
        words = by_word.astype(ml_dtypes.float8_e4m3fn).view(np.uint8)
    else:
        c = by_word.astype(ml_dtypes.float4_e2m1fn).view(np.uint8) & 0xF
        words = (c[..., 0::2] | (c[..., 1::2] << 4)).reshape(k // 512, 128, 2 * n)
    return np.ascontiguousarray(words), np.ascontiguousarray(byte.astype(np.uint8).reshape(k // 512, 16, n))


def unpack_weight(words, scales, fmt):
    g, _, n = scales.shape
    words = np.ascontiguousarray(words).reshape(g, 128, n, -1)
    if fmt == "e4m3":
        vals = words.view(ml_dtypes.float8_e4m3fn).astype(np.float64)
    else:
        nib = np.empty((g, 128, n, 4), np.uint8)
        nib[..., 0::2] = words & 0xF
        nib[..., 1::2] = words >> 4
        vals = E2M1[nib]
    vals = vals * np.repeat(np.exp2(scales.astype(np.float64) - 127.0), 8, axis=1)[..., None]
    return vals.transpose(0, 1, 3, 2).reshape(g * 512, n)


def gelu(v):
    return 0.5 * v * (1.0 + np.tanh(np.sqrt(2.0 / np.pi) * (v + 0.044715 * v**3)))


K, K2, H, N, T, S = 1024, 512, 1024, 512, 2048, 1024


def setup_inputs():
    n = np.random.standard_normal
    s = mx_kscale(K)[:, None]
    s2 = mx_kscale(K2)[:, None]
    u = mx_kscale(H)[:, None]
    d = {}
    d["tab_words"], d["tab_scales"] = pack_weight(n((K, T)) * s, "e4m3")
    d["offs"] = striped(np.random.permutation(T)[:S])
    d["xs_words"], d["xs_scales"] = pack_weight(n((K2, S)) * s2, "e4m3")
    d["w1"] = (1.5 * n((K, H)) / K**0.5 / s * u.T).astype(np.float32)
    d["wd_words"], d["wd_scales"] = pack_weight(1.2 * n((K2, H)) / K2**0.5 / s2, "e2m1")
    d["bd"] = (0.8 * n(H)).astype(np.float32)
    d["ws"] = (0.8 * n((K2, H)) / K2**0.5 / s2 * u.T).astype(np.float32)
    d["wo_words"], d["wo_scales"] = pack_weight(n((H, N)) / H**0.5 / u, "e4m3")
    return d


def reference(tab_words, tab_scales, offs, xs_words, xs_scales, w1, wd_words, wd_scales, bd, ws, wo_words, wo_scales):
    v = unpack_weight(tab_words, tab_scales, "e4m3")[:, unstriped(offs)]
    xs = unpack_weight(xs_words, xs_scales, "e4m3")
    wd = unpack_weight(wd_words, wd_scales, "e2m1")
    wo = unpack_weight(wo_words, wo_scales, "e4m3")
    a = mxq(f64(w1), 0, "e4m3").T @ v
    f = (wd.T @ xs) + f64(bd)[:, None]
    e = mxq(f64(ws), 0, "e4m3").T @ xs
    h = a / (1.0 + np.abs(f)) - e
    return wo.T @ mxq(h, 0, "e4m3")

@@ -1,0 +1,256 @@
+from contextlib import ExitStack
+
+import concourse.mybir as mybir
+
+K, K2, H, N, T, S = 1024, 512, 1024, 512, 2048, 1024
+FLOPS = 2 * S * (K * H + 2 * K2 * H + H * N)
+
+F32 = mybir.dt.float32
+BF16 = mybir.dt.bfloat16
+I32 = mybir.dt.int32
+U32 = mybir.dt.uint32
+U16 = mybir.dt.uint16
+U8 = mybir.dt.uint8
+FP8X4 = mybir.dt.float8_e4m3fn_x4
+FP4X4 = mybir.dt.float4_e2m1fn_x4
+ACT = mybir.ActivationFunctionType
+ALU = mybir.AluOpType
+
+P = 128
+PACK = 4
+PASS = P * PACK
+HALF = 512
+CHUNK = 128
+BLOCKS = H // PASS
+CHUNKS = S // CHUNK
+
+
+def tile_list_kiln_burner_scores_kernel(
+    tc, tab_words, tab_scales, offs, xs_words, xs_scales, w1, wd_words, wd_scales, bd, ws, wo_words, wo_scales, out
+):
+    nc = tc.nc
+    with ExitStack() as ctx:
+        keep = ctx.enter_context(tc.tile_pool(name="keep", bufs=1))
+        ring = ctx.enter_context(tc.tile_pool(name="ring", bufs=1))
+        psum = ctx.enter_context(tc.psum_pool(name="psum", bufs=1))
+
+        offsets = keep.tile([P, S // 16], U16, name="offsets")
+        tab_w = [keep.tile([P, T], I32, name=f"tab_w{a}", align_bytes=64) for a in range(2)]
+        tab_s = keep.tile([P, T], U8, name="tab_s", align_bytes=64)
+        v_w = [keep.tile([P, S], U32, name=f"v_w{a}", align_bytes=64) for a in range(2)]
+        v_s = keep.tile([P, S], U8, name="v_s", align_bytes=64)
+        xs_w = keep.tile([P, S], I32, name="xs_w", align_bytes=64)
+        xs_s = keep.tile([P, S], U8, name="xs_s", align_bytes=64)
+        wd_w_raw = keep.tile([P, 2 * H], U8, name="wd_w_raw", align_bytes=64)
+        wd_s_raw = keep.tile([P, H], U8, name="wd_s_raw", align_bytes=64)
+        wd_w = keep.tile([P, 2 * H], U8, name="wd_w", align_bytes=64)
+        wd_s = keep.tile([P, H], U8, name="wd_s", align_bytes=64)
+        wo_w = keep.tile([P, 2, N], I32, name="wo_w", align_bytes=64)
+        wo_s = keep.tile([P, N], U8, name="wo_s", align_bytes=64)
+        bias = keep.tile([P, BLOCKS, PACK], F32, name="bias")
+        one = keep.tile([P, 1], F32, name="one")
+        warm = keep.tile([P, 1], F32, name="warm")
+
+        nc.vector.memset(wd_s_raw[:].bitcast(I32), 0)
+        nc.vector.memset(tab_s[:].bitcast(I32), 0)
+        nc.gpsimd.memset(one[:], 1.0)
+        nc.gpsimd.memset(xs_s[:].bitcast(I32), 0)
+        nc.gpsimd.memset(wo_s[:].bitcast(I32), 0)
+        nc.scalar.activation(warm[:], one[:], ACT.Abs_reciprocal_sqrt)
+
+        def load_planes(queue, plane, scales):
+            rows = 4 * scales.shape[0]
+            for q in range(4):
+                queue.dma_start(
+                    plane[32 * q : 32 * q + rows, :].bitcast(I32), scales[:, 4 * q : 4 * q + 4, :].bitcast(I32)
+                )
+
+        def words(dram):
+            return dram.rearrange("p n t -> p (n t)").bitcast(I32)
+
+        nc.sync.dma_start(offsets[:], offs)
+        nc.sync.dma_start(wd_w_raw[:].bitcast(I32), wd_words[0].bitcast(I32))
+        nc.sync.dma_start(xs_w[:], words(xs_words[0]))
+        load_planes(nc.sync, wd_s_raw, wd_scales)
+        load_planes(nc.scalar, xs_s, xs_scales)
+        load_planes(nc.sync, tab_s, tab_scales)
+        nc.scalar.dma_start(bias[:], bd.rearrange("(b p t) -> p b t", p=P, t=PACK))
+        for a in range(2):
+            nc.sync.dma_start(tab_w[a][:], words(tab_words[a]))
+
+        raw = {}
+        for b in range(BLOCKS):
+            for name, w, a in (("w1", w1, 0), ("w1", w1, 1), ("ws", ws, 0)):
+                tile = keep.tile([P, PACK, PASS], F32, name=f"raw_{name}_{a}_{b}")
+                rows = w[a * PASS : (a + 1) * PASS, b * PASS : (b + 1) * PASS]
+                nc.sync.dma_start(tile[:], rows.rearrange("(p j) c -> p j c", j=PACK))
+                raw[name, a, b] = tile
+        nc.sync.dma_start(wo_w[:], wo_words.rearrange("a p n t -> p a (n t)").bitcast(I32))
+        load_planes(nc.sync, wo_s, wo_scales)
+
+        nc.vector.tensor_copy(
+            wd_w[:].rearrange("p (t c u) -> p c t u", t=PACK, u=2),
+            wd_w_raw[:].rearrange("p (c t u) -> p c t u", t=PACK, u=2),
+        )
+        nc.vector.tensor_copy(
+            wd_s[:].rearrange("p (t c) -> p c t", t=PACK), wd_s_raw[:].rearrange("p (c t) -> p c t", t=PACK)
+        )
+
+        nc.vector.tensor_copy(v_s[:], tab_s[:].indirect(offsets[:]))
+        for a in range(2):
+            nc.vector.tensor_copy(v_w[a][:], tab_w[a][:].bitcast(U32).indirect(offsets[:]))
+
+        damping = {}
+
+        def make_damping(b, half):
+            cols = slice(half * HALF, (half + 1) * HALF)
+            g = ring.tile([P, PACK, HALF], F32, name="g", bufs=2)
+            for t in range(PACK):
+                first = t * (H // PACK) + b * P
+                f = psum.tile([P, HALF], F32, name="f", tag="f_out", bufs=4)
+                nc.tensor.matmul_mx(
+                    f[:],
+                    lhsT=wd_w[:, 2 * first : 2 * (first + P)].bitcast(FP4X4),
+                    lhsT_scale=wd_s[:, first : first + P],
+                    rhs=xs_w[:, cols].bitcast(FP8X4),
+                    rhs_scale=xs_s[:, cols],
+                    start=True,
+                    stop=True,
+                )
+                nc.scalar.activation(g[:, t, :], f[:], ACT.Abs, bias=bias[:, b, t : t + 1])
+            nc.scalar.activation(g[:], g[:], ACT.Square, bias=one[:])
+            r = ring.tile([P, HALF * PACK], F32, name="r", bufs=3)
+            nc.scalar.activation(
+                r[:].rearrange("p (c i t) -> p c t i", i=4, t=PACK),
+                g[:].rearrange("p t (c i) -> p c t i", i=4),
+                ACT.Abs_reciprocal_sqrt,
+            )
+            damping[b, half] = r
+
+        grouped = {}
+        codes = {}
+
+        def cast(key, copy):
+            tile = ring.tile([P, PASS * PACK], BF16, name="grouped", bufs=3, align_bytes=64)
+            copy(
+                tile[:].rearrange("p (t m j) -> p m j t", t=PACK, j=PACK),
+                raw[key][:].rearrange("p j (m t) -> p m j t", t=PACK),
+            )
+            grouped[key] = tile
+
+        def quantize(key):
+            name, a, b = key
+            w = keep.tile([P, PASS], U32, name=f"q_{name}_{a}_{b}", align_bytes=64)
+            s = keep.tile([P, PASS], U8, name=f"s_{name}_{a}_{b}", align_bytes=64)
+            nc.vector.quantize_mx(w[:].bitcast(FP8X4), s[:], grouped[key][:])
+            codes[key] = (w, s)
+
+        h = [keep.tile([P, S * PACK], BF16, name=f"h{b}", align_bytes=64) for b in range(BLOCKS)]
+        h_w = [keep.tile([P, S], U32, name=f"h_w{b}", align_bytes=64) for b in range(BLOCKS)]
+        h_s = [keep.tile([P, S], U8, name=f"h_s{b}", align_bytes=64) for b in range(BLOCKS)]
+        damped = {}
+
+        def damp(b, c):
+            cols = slice(c * CHUNK, (c + 1) * CHUNK)
+            acc = psum.tile([P, PACK, CHUNK], F32, name="a", bufs=2)
+            for t in range(PACK):
+                for a in range(2):
+                    w, s = codes["w1", a, b]
+                    nc.tensor.matmul_mx(
+                        acc[:, t, :],
+                        lhsT=w[:, t * P : (t + 1) * P].bitcast(FP8X4),
+                        lhsT_scale=s[:, t * P : (t + 1) * P],
+                        rhs=v_w[a][:, cols].bitcast(FP8X4),
+                        rhs_scale=v_s[4 * a :, cols],
+                        start=(a == 0),
+                        stop=(a == 1),
+                    )
+            half, inside = divmod(c * CHUNK, HALF)
+            r = damping[b, half][:, inside * PACK : (inside + CHUNK) * PACK]
+            tile = ring.tile([P, CHUNK, PACK], F32, name="damped", bufs=3)
+            nc.vector.tensor_tensor(
+                tile[:], acc[:].rearrange("p t j -> p j t"), r.rearrange("p (j t) -> p j t", t=PACK), ALU.mult
+            )
+            damped[b, c] = tile
+
+        def offset(b, c):
+            cols = slice(c * CHUNK, (c + 1) * CHUNK)
+            acc = psum.tile([P, PACK, CHUNK], F32, name="e", bufs=2)
+            w, s = codes["ws", 0, b]
+            for t in range(PACK):
+                nc.tensor.matmul_mx(
+                    acc[:, t, :],
+                    lhsT=w[:, t * P : (t + 1) * P].bitcast(FP8X4),
+                    lhsT_scale=s[:, t * P : (t + 1) * P],
+                    rhs=xs_w[:, cols].bitcast(FP8X4),
+                    rhs_scale=xs_s[:, cols],
+                    start=True,
+                    stop=True,
+                )
+            dst = h[b][:, c * CHUNK * PACK : (c + 1) * CHUNK * PACK]
+            nc.vector.tensor_tensor(
+                dst.rearrange("p (j t) -> p j t", t=PACK),
+                damped[b, c][:],
+                acc[:].rearrange("p t j -> p j t"),
+                ALU.subtract,
+            )
+
+        def quantize_h(b, first, last):
+            nc.vector.quantize_mx(
+                h_w[b][:, first:last].bitcast(FP8X4), h_s[b][:, first:last], h[b][:, first * PACK : last * PACK]
+            )
+
+        def scores(c):
+            cols = slice(c * CHUNK, (c + 1) * CHUNK)
+            acc = psum.tile([P, N // P, CHUNK], F32, name="o", tag="f_out", bufs=4)
+            for n in range(N // P):
+                for b in range(BLOCKS):
+                    nc.tensor.matmul_mx(
+                        acc[:, n, :],
+                        lhsT=wo_w[:, b, n * P : (n + 1) * P].bitcast(FP8X4),
+                        lhsT_scale=wo_s[4 * b :, n * P : (n + 1) * P],
+                        rhs=h_w[b][:, cols].bitcast(FP8X4),
+                        rhs_scale=h_s[b][:, cols],
+                        start=(b == 0),
+                        stop=(b == BLOCKS - 1),
+                    )
+            tile = ring.tile([P, N // P, CHUNK], F32, name="staged", bufs=4)
+            nc.scalar.copy(tile[:], acc[:])
+            nc.sync.dma_start(out.rearrange("(n p) j -> p n j", p=P)[:, :, cols], tile[:])
+
+        make_damping(0, 0)
+        make_damping(0, 1)
+        cast(("w1", 0, 0), nc.vector.tensor_copy)
+        cast(("w1", 1, 0), nc.vector.tensor_copy)
+        quantize(("w1", 0, 0))
+        cast(("ws", 0, 0), nc.vector.tensor_copy)
+        quantize(("w1", 1, 0))
+        quantize(("ws", 0, 0))
+        cast(("w1", 0, 1), nc.scalar.copy)
+        make_damping(1, 0)
+        make_damping(1, 1)
+
+        damp(0, 0)
+        for c in range(CHUNKS):
+            if c + 1 < CHUNKS:
+                damp(0, c + 1)
+            offset(0, c)
+            if c == 4:
+                quantize_h(0, 0, HALF)
+                cast(("w1", 1, 1), nc.vector.tensor_copy)
+                quantize(("w1", 0, 1))
+                cast(("ws", 0, 1), nc.vector.tensor_copy)
+                quantize(("w1", 1, 1))
+            if c == 5:
+                quantize(("ws", 0, 1))
+        damp(1, 0)
+        quantize_h(0, HALF, S)
+        for c in range(CHUNKS):
+            if c + 1 < CHUNKS:
+                damp(1, c + 1)
+            offset(1, c)
+            if c > 0:
+                quantize_h(1, (c - 1) * CHUNK, c * CHUNK)
+                scores(c - 1)
+        quantize_h(1, S - CHUNK, S)
+        scores(CHUNKS - 1)

@@ -31,7 +31,6 @@ def tile_list_kiln_burner_scores_kernel(
     nc = tc.nc
     with ExitStack() as ctx:
         keep = ctx.enter_context(tc.tile_pool(name="keep", bufs=1))
-        ring = ctx.enter_context(tc.tile_pool(name="ring", bufs=1))
         psum = ctx.enter_context(tc.psum_pool(name="psum", bufs=1))
 
         offsets = keep.tile([P, S // 16], U16, name="offsets")
@@ -39,7 +38,7 @@ def tile_list_kiln_burner_scores_kernel(
         tab_s = keep.tile([P, T], U8, name="tab_s", align_bytes=64)
         v_w = [keep.tile([P, S], U32, name=f"v_w{a}", align_bytes=64) for a in range(2)]
         v_s = keep.tile([P, S], U8, name="v_s", align_bytes=64)
-        xs_w = keep.tile([P, S], I32, name="xs_w", align_bytes=64)
+        xs_w = [keep.tile([P, HALF], I32, name=f"xs_w{half}", align_bytes=64) for half in range(2)]
         xs_s = keep.tile([P, S], U8, name="xs_s", align_bytes=64)
         wd_w_raw = keep.tile([P, 2 * H], U8, name="wd_w_raw", align_bytes=64)
         wd_s_raw = keep.tile([P, H], U8, name="wd_s_raw", align_bytes=64)
@@ -48,33 +47,50 @@ def tile_list_kiln_burner_scores_kernel(
         wo_w = keep.tile([P, 2, N], I32, name="wo_w", align_bytes=64)
         wo_s = keep.tile([P, N], U8, name="wo_s", align_bytes=64)
         bias = keep.tile([P, BLOCKS, PACK], F32, name="bias")
+        unit = keep.tile([P, 1], F32, name="unit")
         one = keep.tile([P, 1], F32, name="one")
-        warm = keep.tile([P, 1], F32, name="warm")
 
-        nc.vector.memset(wd_s_raw[:].bitcast(I32), 0)
-        nc.vector.memset(tab_s[:].bitcast(I32), 0)
-        nc.gpsimd.memset(one[:], 1.0)
-        nc.gpsimd.memset(xs_s[:].bitcast(I32), 0)
+        def in_turn(pool, name, count, width, dtype):
+            return [pool.tile([P, width], dtype, name=f"{name}{k}", align_bytes=64) for k in range(count)]
+
+        a_banks = [psum.tile([P, HALF], F32, name=f"a{k}") for k in range(2)]
+        e_banks = [psum.tile([P, HALF], F32, name=f"e{k}") for k in range(2)]
+        s_banks = [psum.tile([P, HALF], F32, name=f"s{k}") for k in range(4)]
+        a_turn, e_turn, s_turn = list(a_banks), list(e_banks), list(s_banks)
+        g_turn = in_turn(keep, "g", 3, PACK * HALF, F32)
+        grouped_turn = in_turn(keep, "grouped", 3, PACK * PASS, BF16)
+        damped_turn = in_turn(keep, "damped", 4, PACK * CHUNK, F32)
+        staged_turn = in_turn(keep, "staged", 4, HALF, F32)
+
+        def take(turn):
+            turn[:] = turn[1:] + turn[:1]
+            return turn[-1]
+
+        nc.gpsimd.memset(wd_s_raw[:].bitcast(I32), 0)
+        nc.vector.memset(xs_s[:].bitcast(I32), 0)
+        nc.gpsimd.memset(tab_s[:].bitcast(I32), 0)
         nc.gpsimd.memset(wo_s[:].bitcast(I32), 0)
-        nc.scalar.activation(warm[:], one[:], ACT.Abs_reciprocal_sqrt)
+        nc.vector.memset(unit[:], 1.0)
+        nc.scalar.activation(one[:], unit[:], ACT.Abs_reciprocal_sqrt)
 
-        def load_planes(queue, plane, scales):
+        def load_planes(plane, scales, quadrants=range(4)):
             rows = 4 * scales.shape[0]
-            for q in range(4):
-                queue.dma_start(
+            for q in quadrants:
+                nc.sync.dma_start(
                     plane[32 * q : 32 * q + rows, :].bitcast(I32), scales[:, 4 * q : 4 * q + 4, :].bitcast(I32)
                 )
 
         def words(dram):
             return dram.rearrange("p n t -> p (n t)").bitcast(I32)
 
-        nc.sync.dma_start(offsets[:], offs)
+        load_planes(wd_s_raw, wd_scales)
+        load_planes(xs_s, xs_scales, range(2))
         nc.sync.dma_start(wd_w_raw[:].bitcast(I32), wd_words[0].bitcast(I32))
-        nc.sync.dma_start(xs_w[:], words(xs_words[0]))
-        load_planes(nc.sync, wd_s_raw, wd_scales)
-        load_planes(nc.scalar, xs_s, xs_scales)
-        load_planes(nc.sync, tab_s, tab_scales)
-        nc.scalar.dma_start(bias[:], bd.rearrange("(b p t) -> p b t", p=P, t=PACK))
+        nc.sync.dma_start(xs_w[0][:], words(xs_words[0])[:, :HALF])
+        load_planes(xs_s, xs_scales, range(2, 4))
+        nc.sync.dma_start(bias[:], bd.rearrange("(b p t) -> p b t", p=P, t=PACK))
+        nc.sync.dma_start(offsets[:], offs)
+        load_planes(tab_s, tab_scales)
         for a in range(2):
             nc.sync.dma_start(tab_w[a][:], words(tab_words[a]))
 
@@ -85,53 +101,61 @@ def tile_list_kiln_burner_scores_kernel(
                 rows = w[a * PASS : (a + 1) * PASS, b * PASS : (b + 1) * PASS]
                 nc.sync.dma_start(tile[:], rows.rearrange("(p j) c -> p j c", j=PACK))
                 raw[name, a, b] = tile
+            if b == 0:
+                nc.sync.dma_start(xs_w[1][:], words(xs_words[0])[:, HALF:])
         nc.sync.dma_start(wo_w[:], wo_words.rearrange("a p n t -> p a (n t)").bitcast(I32))
-        load_planes(nc.sync, wo_s, wo_scales)
+        load_planes(wo_s, wo_scales)
 
-        nc.vector.tensor_copy(
-            wd_w[:].rearrange("p (t c u) -> p c t u", t=PACK, u=2),
-            wd_w_raw[:].rearrange("p (c t u) -> p c t u", t=PACK, u=2),
-        )
-        nc.vector.tensor_copy(
-            wd_s[:].rearrange("p (t c) -> p c t", t=PACK), wd_s_raw[:].rearrange("p (c t) -> p c t", t=PACK)
-        )
+        for b in range(BLOCKS):
+            for dst, src in ((wd_w[:].bitcast(U16), wd_w_raw[:].bitcast(U16)), (wd_s[:], wd_s_raw[:])):
+                nc.vector.tensor_copy(
+                    dst.rearrange("p (t c) -> p c t", t=PACK)[:, b * P : (b + 1) * P, :],
+                    src.rearrange("p (c t) -> p c t", t=PACK)[:, b * P : (b + 1) * P, :],
+                )
 
         nc.vector.tensor_copy(v_s[:], tab_s[:].indirect(offsets[:]))
         for a in range(2):
             nc.vector.tensor_copy(v_w[a][:], tab_w[a][:].bitcast(U32).indirect(offsets[:]))
 
-        damping = {}
+        magnitude = {}
+        factor = {}
 
-        def make_damping(b, half):
+        def magnitudes(b, half):
             cols = slice(half * HALF, (half + 1) * HALF)
-            g = ring.tile([P, PACK, HALF], F32, name="g", bufs=2)
+            g = take(g_turn)[:].rearrange("p (t j) -> p t j", t=PACK)
             for t in range(PACK):
                 first = t * (H // PACK) + b * P
-                f = psum.tile([P, HALF], F32, name="f", tag="f_out", bufs=4)
+                f = take(s_turn)
                 nc.tensor.matmul_mx(
                     f[:],
                     lhsT=wd_w[:, 2 * first : 2 * (first + P)].bitcast(FP4X4),
                     lhsT_scale=wd_s[:, first : first + P],
-                    rhs=xs_w[:, cols].bitcast(FP8X4),
+                    rhs=xs_w[half][:].bitcast(FP8X4),
                     rhs_scale=xs_s[:, cols],
                     start=True,
                     stop=True,
                 )
                 nc.scalar.activation(g[:, t, :], f[:], ACT.Abs, bias=bias[:, b, t : t + 1])
-            nc.scalar.activation(g[:], g[:], ACT.Square, bias=one[:])
-            r = ring.tile([P, HALF * PACK], F32, name="r", bufs=3)
+            magnitude[b, half] = g
+
+        def factors(b, c0, count):
+            half, inside = divmod(c0 * CHUNK, HALF)
+            g = magnitude[b, half][:, :, inside : inside + count * CHUNK]
+            nc.scalar.activation(g, g, ACT.Square, bias=one[:])
+            r = keep.tile([P, count * CHUNK * PACK], F32, name=f"r_{b}_{c0}")
             nc.scalar.activation(
                 r[:].rearrange("p (c i t) -> p c t i", i=4, t=PACK),
-                g[:].rearrange("p t (c i) -> p c t i", i=4),
+                g.rearrange("p t (c i) -> p c t i", i=4),
                 ACT.Abs_reciprocal_sqrt,
             )
-            damping[b, half] = r
+            for k in range(count):
+                factor[b, c0 + k] = r[:, k * CHUNK * PACK : (k + 1) * CHUNK * PACK]
 
         grouped = {}
         codes = {}
 
         def cast(key, copy):
-            tile = ring.tile([P, PASS * PACK], BF16, name="grouped", bufs=3, align_bytes=64)
+            tile = take(grouped_turn)
             copy(
                 tile[:].rearrange("p (t m j) -> p m j t", t=PACK, j=PACK),
                 raw[key][:].rearrange("p j (m t) -> p m j t", t=PACK),
@@ -152,7 +176,7 @@ def tile_list_kiln_burner_scores_kernel(
 
         def damp(b, c):
             cols = slice(c * CHUNK, (c + 1) * CHUNK)
-            acc = psum.tile([P, PACK, CHUNK], F32, name="a", bufs=2)
+            acc = take(a_turn)[:].rearrange("p (t j) -> p t j", t=PACK)
             for t in range(PACK):
                 for a in range(2):
                     w, s = codes["w1", a, b]
@@ -165,24 +189,24 @@ def tile_list_kiln_burner_scores_kernel(
                         start=(a == 0),
                         stop=(a == 1),
                     )
-            half, inside = divmod(c * CHUNK, HALF)
-            r = damping[b, half][:, inside * PACK : (inside + CHUNK) * PACK]
-            tile = ring.tile([P, CHUNK, PACK], F32, name="damped", bufs=3)
+            r = factor[b, c]
+            tile = take(damped_turn)[:].rearrange("p (j t) -> p j t", t=PACK)
             nc.vector.tensor_tensor(
-                tile[:], acc[:].rearrange("p t j -> p j t"), r.rearrange("p (j t) -> p j t", t=PACK), ALU.mult
+                tile, acc.rearrange("p t j -> p j t"), r.rearrange("p (j t) -> p j t", t=PACK), ALU.mult
             )
             damped[b, c] = tile
 
         def offset(b, c):
             cols = slice(c * CHUNK, (c + 1) * CHUNK)
-            acc = psum.tile([P, PACK, CHUNK], F32, name="e", bufs=2)
+            acc = take(e_turn)[:].rearrange("p (t j) -> p t j", t=PACK)
             w, s = codes["ws", 0, b]
+            half, inside = divmod(c * CHUNK, HALF)
             for t in range(PACK):
                 nc.tensor.matmul_mx(
                     acc[:, t, :],
                     lhsT=w[:, t * P : (t + 1) * P].bitcast(FP8X4),
                     lhsT_scale=s[:, t * P : (t + 1) * P],
-                    rhs=xs_w[:, cols].bitcast(FP8X4),
+                    rhs=xs_w[half][:, inside : inside + CHUNK].bitcast(FP8X4),
                     rhs_scale=xs_s[:, cols],
                     start=True,
                     stop=True,
@@ -190,67 +214,115 @@ def tile_list_kiln_burner_scores_kernel(
             dst = h[b][:, c * CHUNK * PACK : (c + 1) * CHUNK * PACK]
             nc.vector.tensor_tensor(
                 dst.rearrange("p (j t) -> p j t", t=PACK),
-                damped[b, c][:],
-                acc[:].rearrange("p t j -> p j t"),
+                damped[b, c],
+                acc.rearrange("p t j -> p j t"),
                 ALU.subtract,
             )
 
-        def quantize_h(b, first, last):
+        def quantize_h(b, c0, count):
+            first, last = c0 * CHUNK, (c0 + count) * CHUNK
             nc.vector.quantize_mx(
                 h_w[b][:, first:last].bitcast(FP8X4), h_s[b][:, first:last], h[b][:, first * PACK : last * PACK]
             )
 
-        def scores(c):
+        out_rows = out.rearrange("(n p) j -> p n j", p=P)
+
+        def score_pass(acc, n, b, cols, start, stop):
+            nc.tensor.matmul_mx(
+                acc,
+                lhsT=wo_w[:, b, n * P : (n + 1) * P].bitcast(FP8X4),
+                lhsT_scale=wo_s[4 * b :, n * P : (n + 1) * P],
+                rhs=h_w[b][:, cols].bitcast(FP8X4),
+                rhs_scale=h_s[b][:, cols],
+                start=start,
+                stop=stop,
+            )
+
+        def scores(c0, count):
+            width = count * CHUNK
+            cols = slice(c0 * CHUNK, c0 * CHUNK + width)
+            per_bank = HALF // width
+            for n0 in range(0, N // P, per_bank):
+                acc = take(s_turn)
+                for k in range(per_bank):
+                    for b in range(BLOCKS):
+                        score_pass(acc[:, k * width : (k + 1) * width], n0 + k, b, cols, b == 0, b == BLOCKS - 1)
+                tile = take(staged_turn)
+                nc.scalar.copy(tile[:], acc[:])
+                nc.sync.dma_start(
+                    out_rows[:, n0 : n0 + per_bank, cols], tile[:].rearrange("p (n j) -> p n j", n=per_bank)
+                )
+
+        def block_passes(acc, tiles, b, c):
             cols = slice(c * CHUNK, (c + 1) * CHUNK)
-            acc = psum.tile([P, N // P, CHUNK], F32, name="o", tag="f_out", bufs=4)
-            for n in range(N // P):
-                for b in range(BLOCKS):
-                    nc.tensor.matmul_mx(
-                        acc[:, n, :],
-                        lhsT=wo_w[:, b, n * P : (n + 1) * P].bitcast(FP8X4),
-                        lhsT_scale=wo_s[4 * b :, n * P : (n + 1) * P],
-                        rhs=h_w[b][:, cols].bitcast(FP8X4),
-                        rhs_scale=h_s[b][:, cols],
-                        start=(b == 0),
-                        stop=(b == BLOCKS - 1),
-                    )
-            tile = ring.tile([P, N // P, CHUNK], F32, name="staged", bufs=4)
-            nc.scalar.copy(tile[:], acc[:])
-            nc.sync.dma_start(out.rearrange("(n p) j -> p n j", p=P)[:, :, cols], tile[:])
+            for k, n in enumerate(tiles):
+                first = b == 0 and k == 0
+                final = b == BLOCKS - 1 and k == len(tiles) - 1
+                score_pass(acc[:, k * CHUNK : (k + 1) * CHUNK], n, b, cols, first, final)
 
-        make_damping(0, 0)
-        make_damping(0, 1)
-        cast(("w1", 0, 0), nc.vector.tensor_copy)
-        cast(("w1", 1, 0), nc.vector.tensor_copy)
-        quantize(("w1", 0, 0))
-        cast(("ws", 0, 0), nc.vector.tensor_copy)
-        quantize(("w1", 1, 0))
-        quantize(("ws", 0, 0))
-        cast(("w1", 0, 1), nc.scalar.copy)
-        make_damping(1, 0)
-        make_damping(1, 1)
+        def store(acc, tiles, c, copy, queue):
+            width = len(tiles) * CHUNK
+            tile = take(staged_turn)[:, :width]
+            copy(tile, acc[:, :width])
+            queue.dma_start(
+                out_rows[:, tiles[0] : tiles[-1] + 1, c * CHUNK : (c + 1) * CHUNK],
+                tile.rearrange("p (n j) -> p n j", j=CHUNK),
+            )
 
-        damp(0, 0)
-        for c in range(CHUNKS):
-            if c + 1 < CHUNKS:
-                damp(0, c + 1)
-            offset(0, c)
-            if c == 4:
-                quantize_h(0, 0, HALF)
-                cast(("w1", 1, 1), nc.vector.tensor_copy)
-                quantize(("w1", 0, 1))
-                cast(("ws", 0, 1), nc.vector.tensor_copy)
-                quantize(("w1", 1, 1))
-            if c == 5:
-                quantize(("ws", 0, 1))
-        damp(1, 0)
-        quantize_h(0, HALF, S)
-        for c in range(CHUNKS):
-            if c + 1 < CHUNKS:
-                damp(1, c + 1)
-            offset(1, c)
-            if c > 0:
-                quantize_h(1, (c - 1) * CHUNK, c * CHUNK)
-                scores(c - 1)
-        quantize_h(1, S - CHUNK, S)
-        scores(CHUNKS - 1)
+        keys = [[("w1", 0, b), ("w1", 1, b), ("ws", 0, b)] for b in range(BLOCKS)]
+
+        magnitudes(0, 0)
+        factors(0, 0, 4)
+        magnitudes(1, 0)
+        factors(1, 0, 4)
+        for key in keys[0]:
+            cast(key, nc.vector.tensor_copy)
+            quantize(key)
+        for key, copy in zip(keys[1], (nc.scalar.copy, nc.scalar.copy, nc.vector.tensor_copy)):
+            cast(key, copy)
+            quantize(key)
+        magnitudes(0, 1)
+        factors(0, 4, 2)
+        magnitudes(1, 1)
+        factors(1, 4, 2)
+
+        order = [(0, 0), (0, 1), (0, 2), (0, 3), (1, 0), (1, 1), (1, 2), (1, 3)]
+        order = order + [(0, 4), (0, 5), (1, 4), (1, 5), (0, 6), (0, 7), (1, 6), (1, 7)]
+        damp(*order[0])
+        for i, (b, c) in enumerate(order[:-2]):
+            damp(*order[i + 1])
+            offset(b, c)
+            if (b, c) == (0, 3):
+                quantize_h(0, 0, 4)
+            if (b, c) == (1, 1):
+                quantize_h(1, 0, 2)
+            if (b, c) == (1, 2):
+                scores(0, 2)
+            if (b, c) == (1, 3):
+                quantize_h(1, 2, 2)
+                factors(0, 6, 2)
+            if (b, c) == (0, 4):
+                factors(1, 6, 1)
+                factors(1, 7, 1)
+                scores(2, 2)
+            if (b, c) == (0, 5):
+                quantize_h(0, 4, 2)
+        quantize_h(1, 4, 2)
+        scores(4, 2)
+        quantize_h(0, 6, 2)
+        offset(1, 6)
+        damp(1, 7)
+        bank = take(s_turn)
+        block_passes(bank, [0, 1, 2, 3], 0, 6)
+        ends = [(take(a_turn), [0, 1]), (take(a_turn), [2, 3])]
+        for acc, tiles in ends:
+            block_passes(acc, tiles, 0, 7)
+        quantize_h(1, 6, 1)
+        block_passes(bank, [0, 1, 2, 3], 1, 6)
+        store(bank, [0, 1, 2, 3], 6, nc.scalar.copy, nc.sync)
+        offset(1, 7)
+        quantize_h(1, 7, 1)
+        for acc, tiles in ends:
+            block_passes(acc, tiles, 1, 7)
+        store(*ends[0], 7, nc.vector.tensor_copy, nc.sync)
+        store(*ends[1], 7, nc.scalar.copy, nc.scalar)

@@ -53,11 +53,10 @@ def tile_list_kiln_burner_scores_kernel(
         def in_turn(pool, name, count, width, dtype):
             return [pool.tile([P, width], dtype, name=f"{name}{k}", align_bytes=64) for k in range(count)]
 
-        a_banks = [psum.tile([P, HALF], F32, name=f"a{k}") for k in range(2)]
-        e_banks = [psum.tile([P, HALF], F32, name=f"e{k}") for k in range(2)]
-        s_banks = [psum.tile([P, HALF], F32, name=f"s{k}") for k in range(4)]
-        a_turn, e_turn, s_turn = list(a_banks), list(e_banks), list(s_banks)
-        g_turn = in_turn(keep, "g", 3, PACK * HALF, F32)
+        banks = [psum.tile([P, HALF], F32, name=f"bank{k}") for k in range(8)]
+        a_turn, e_turn, s_turn = banks[0:3], banks[3:6], banks[6:8]
+        f_turn = [banks[6], banks[7], banks[5], banks[2]]
+        g_turn = in_turn(keep, "g", 4, PACK * HALF, F32)
         grouped_turn = in_turn(keep, "grouped", 3, PACK * PASS, BF16)
         damped_turn = in_turn(keep, "damped", 4, PACK * CHUNK, F32)
         staged_turn = in_turn(keep, "staged", 4, HALF, F32)
@@ -94,6 +93,7 @@ def tile_list_kiln_burner_scores_kernel(
         for a in range(2):
             nc.sync.dma_start(tab_w[a][:], words(tab_words[a]))
 
+        nc.sync.dma_start(xs_w[1][:], words(xs_words[0])[:, HALF:])
         raw = {}
         for b in range(BLOCKS):
             for name, w, a in (("w1", w1, 0), ("w1", w1, 1), ("ws", ws, 0)):
@@ -101,8 +101,6 @@ def tile_list_kiln_burner_scores_kernel(
                 rows = w[a * PASS : (a + 1) * PASS, b * PASS : (b + 1) * PASS]
                 nc.sync.dma_start(tile[:], rows.rearrange("(p j) c -> p j c", j=PACK))
                 raw[name, a, b] = tile
-            if b == 0:
-                nc.sync.dma_start(xs_w[1][:], words(xs_words[0])[:, HALF:])
         nc.sync.dma_start(wo_w[:], wo_words.rearrange("a p n t -> p a (n t)").bitcast(I32))
         load_planes(wo_s, wo_scales)
 
@@ -125,7 +123,7 @@ def tile_list_kiln_burner_scores_kernel(
             g = take(g_turn)[:].rearrange("p (t j) -> p t j", t=PACK)
             for t in range(PACK):
                 first = t * (H // PACK) + b * P
-                f = take(s_turn)
+                f = take(f_turn)
                 nc.tensor.matmul_mx(
                     f[:],
                     lhsT=wd_w[:, 2 * first : 2 * (first + P)].bitcast(FP4X4),
@@ -138,10 +136,16 @@ def tile_list_kiln_burner_scores_kernel(
                 nc.scalar.activation(g[:, t, :], f[:], ACT.Abs, bias=bias[:, b, t : t + 1])
             magnitude[b, half] = g
 
-        def factors(b, c0, count):
+        def piece(b, c0, count):
             half, inside = divmod(c0 * CHUNK, HALF)
-            g = magnitude[b, half][:, :, inside : inside + count * CHUNK]
+            return magnitude[b, half][:, :, inside : inside + count * CHUNK]
+
+        def squares(b, c0, count):
+            g = piece(b, c0, count)
             nc.scalar.activation(g, g, ACT.Square, bias=one[:])
+
+        def factors(b, c0, count):
+            g = piece(b, c0, count)
             r = keep.tile([P, count * CHUNK * PACK], F32, name=f"r_{b}_{c0}")
             nc.scalar.activation(
                 r[:].rearrange("p (c i t) -> p c t i", i=4, t=PACK),
@@ -272,47 +276,64 @@ def tile_list_kiln_burner_scores_kernel(
         keys = [[("w1", 0, b), ("w1", 1, b), ("ws", 0, b)] for b in range(BLOCKS)]
 
         magnitudes(0, 0)
-        factors(0, 0, 4)
+        squares(0, 0, 2)
         magnitudes(1, 0)
-        factors(1, 0, 4)
+        factors(0, 0, 2)
+        magnitudes(0, 1)
+        magnitudes(1, 1)
         for key in keys[0]:
             cast(key, nc.vector.tensor_copy)
             quantize(key)
-        for key, copy in zip(keys[1], (nc.scalar.copy, nc.scalar.copy, nc.vector.tensor_copy)):
-            cast(key, copy)
-            quantize(key)
-        magnitudes(0, 1)
+        squares(0, 2, 2)
+        squares(0, 4, 2)
+        factors(0, 2, 2)
+        squares(1, 0, 2)
         factors(0, 4, 2)
-        magnitudes(1, 1)
+        factors(1, 0, 2)
+        cast(keys[1][1], nc.scalar.copy)
+        squares(1, 2, 2)
+        cast(keys[1][2], nc.scalar.copy)
+        factors(1, 2, 2)
+        squares(1, 4, 2)
+        squares(0, 6, 2)
         factors(1, 4, 2)
+        squares(1, 6, 2)
 
-        order = [(0, 0), (0, 1), (0, 2), (0, 3), (1, 0), (1, 1), (1, 2), (1, 3)]
-        order = order + [(0, 4), (0, 5), (1, 4), (1, 5), (0, 6), (0, 7), (1, 6), (1, 7)]
+        order = [(0, c) for c in range(6)] + [(1, c) for c in range(6)] + [(0, 6), (0, 7), (1, 6), (1, 7)]
         damp(*order[0])
         for i, (b, c) in enumerate(order[:-2]):
+            if (b, c) == (0, 2):
+                cast(keys[1][0], nc.vector.tensor_copy)
+            if (b, c) == (0, 3):
+                quantize(keys[1][0])
+            if (b, c) == (0, 4):
+                quantize(keys[1][1])
+            if (b, c) == (0, 5):
+                quantize(keys[1][2])
             damp(*order[i + 1])
             offset(b, c)
             if (b, c) == (0, 3):
                 quantize_h(0, 0, 4)
+            if (b, c) == (0, 5):
+                quantize_h(0, 4, 2)
             if (b, c) == (1, 1):
                 quantize_h(1, 0, 2)
+                factors(0, 6, 2)
             if (b, c) == (1, 2):
                 scores(0, 2)
             if (b, c) == (1, 3):
                 quantize_h(1, 2, 2)
-                factors(0, 6, 2)
-            if (b, c) == (0, 4):
-                factors(1, 6, 1)
-                factors(1, 7, 1)
+                factors(1, 6, 2)
+            if (b, c) == (1, 4):
                 scores(2, 2)
-            if (b, c) == (0, 5):
-                quantize_h(0, 4, 2)
-        quantize_h(1, 4, 2)
-        scores(4, 2)
+            if (b, c) == (1, 5):
+                quantize_h(1, 4, 2)
+            if (b, c) == (0, 6):
+                scores(4, 2)
         quantize_h(0, 6, 2)
         offset(1, 6)
         damp(1, 7)
-        bank = take(s_turn)
+        bank = take(e_turn)
         block_passes(bank, [0, 1, 2, 3], 0, 6)
         ends = [(take(a_turn), [0, 1]), (take(a_turn), [2, 3])]
         for acc, tiles in ends:

@@ -55,9 +55,10 @@ def tile_list_kiln_burner_scores_kernel(
 
         banks = [psum.tile([P, HALF], F32, name=f"bank{k}") for k in range(8)]
         a_turn, e_turn, s_turn = banks[0:3], banks[3:6], banks[6:8]
-        f_turn = [banks[6], banks[7], banks[5], banks[2]]
+        f_turn = [banks[6], banks[7], banks[5], banks[4]]
         g_turn = in_turn(keep, "g", 4, PACK * HALF, F32)
-        grouped_turn = in_turn(keep, "grouped", 3, PACK * PASS, BF16)
+        grouped_turn = in_turn(keep, "grouped", 2, PACK * PASS, BF16)
+        rooms = in_turn(keep, "room", 2, PACK * 2 * CHUNK, F32)
         damped_turn = in_turn(keep, "damped", 4, PACK * CHUNK, F32)
         staged_turn = in_turn(keep, "staged", 4, HALF, F32)
 
@@ -88,18 +89,20 @@ def tile_list_kiln_burner_scores_kernel(
         nc.sync.dma_start(xs_w[0][:], words(xs_words[0])[:, :HALF])
         load_planes(xs_s, xs_scales, range(2, 4))
         nc.sync.dma_start(bias[:], bd.rearrange("(b p t) -> p b t", p=P, t=PACK))
+        nc.sync.dma_start(xs_w[1][:], words(xs_words[0])[:, HALF:])
         nc.sync.dma_start(offsets[:], offs)
         load_planes(tab_s, tab_scales)
         for a in range(2):
             nc.sync.dma_start(tab_w[a][:], words(tab_words[a]))
 
-        nc.sync.dma_start(xs_w[1][:], words(xs_words[0])[:, HALF:])
         raw = {}
         for b in range(BLOCKS):
             for name, w, a in (("w1", w1, 0), ("w1", w1, 1), ("ws", ws, 0)):
-                tile = keep.tile([P, PACK, PASS], F32, name=f"raw_{name}_{a}_{b}")
+                tile = keep.tile([P, PACK * PASS], F32, name=f"raw_{name}_{a}_{b}", align_bytes=64)
                 rows = w[a * PASS : (a + 1) * PASS, b * PASS : (b + 1) * PASS]
-                nc.sync.dma_start(tile[:], rows.rearrange("(p j) c -> p j c", j=PACK))
+                nc.sync.dma_start(
+                    tile[:].rearrange("p (j c) -> p j c", j=PACK), rows.rearrange("(p j) c -> p j c", j=PACK)
+                )
                 raw[name, a, b] = tile
         nc.sync.dma_start(wo_w[:], wo_words.rearrange("a p n t -> p a (n t)").bitcast(I32))
         load_planes(wo_s, wo_scales)
@@ -117,6 +120,8 @@ def tile_list_kiln_burner_scores_kernel(
 
         magnitude = {}
         factor = {}
+        factor_tile = {}
+        squared = {}
 
         def magnitudes(b, half):
             cols = slice(half * HALF, (half + 1) * HALF)
@@ -140,13 +145,15 @@ def tile_list_kiln_burner_scores_kernel(
             half, inside = divmod(c0 * CHUNK, HALF)
             return magnitude[b, half][:, :, inside : inside + count * CHUNK]
 
-        def squares(b, c0, count):
-            g = piece(b, c0, count)
-            nc.scalar.activation(g, g, ACT.Square, bias=one[:])
+        def squares(b, c0, count, room):
+            square = room.rearrange("p (t j) -> p t j", t=PACK)
+            nc.scalar.activation(square, piece(b, c0, count), ACT.Square, bias=one[:])
+            squared[b, c0] = square
 
         def factors(b, c0, count):
-            g = piece(b, c0, count)
-            r = keep.tile([P, count * CHUNK * PACK], F32, name=f"r_{b}_{c0}")
+            g = squared[b, c0]
+            r = keep.tile([P, count * CHUNK * PACK], F32, name=f"r_{b}_{c0}", align_bytes=64)
+            factor_tile[b, c0] = r
             nc.scalar.activation(
                 r[:].rearrange("p (c i t) -> p c t i", i=4, t=PACK),
                 g.rearrange("p t (c i) -> p c t i", i=4),
@@ -158,11 +165,10 @@ def tile_list_kiln_burner_scores_kernel(
         grouped = {}
         codes = {}
 
-        def cast(key, copy):
-            tile = take(grouped_turn)
+        def cast(key, copy, tile):
             copy(
-                tile[:].rearrange("p (t m j) -> p m j t", t=PACK, j=PACK),
-                raw[key][:].rearrange("p j (m t) -> p m j t", t=PACK),
+                tile.rearrange("p (t m j) -> p m j t", t=PACK, j=PACK),
+                raw[key][:].rearrange("p (j m t) -> p m j t", j=PACK, t=PACK),
             )
             grouped[key] = tile
 
@@ -170,7 +176,7 @@ def tile_list_kiln_burner_scores_kernel(
             name, a, b = key
             w = keep.tile([P, PASS], U32, name=f"q_{name}_{a}_{b}", align_bytes=64)
             s = keep.tile([P, PASS], U8, name=f"s_{name}_{a}_{b}", align_bytes=64)
-            nc.vector.quantize_mx(w[:].bitcast(FP8X4), s[:], grouped[key][:])
+            nc.vector.quantize_mx(w[:].bitcast(FP8X4), s[:], grouped[key])
             codes[key] = (w, s)
 
         h = [keep.tile([P, S * PACK], BF16, name=f"h{b}", align_bytes=64) for b in range(BLOCKS)]
@@ -178,11 +184,11 @@ def tile_list_kiln_burner_scores_kernel(
         h_s = [keep.tile([P, S], U8, name=f"h_s{b}", align_bytes=64) for b in range(BLOCKS)]
         damped = {}
 
-        def damp(b, c):
+        def damp(b, c, tile=None):
             cols = slice(c * CHUNK, (c + 1) * CHUNK)
             acc = take(a_turn)[:].rearrange("p (t j) -> p t j", t=PACK)
-            for t in range(PACK):
-                for a in range(2):
+            for a in range(2):
+                for t in range(PACK):
                     w, s = codes["w1", a, b]
                     nc.tensor.matmul_mx(
                         acc[:, t, :],
@@ -190,11 +196,12 @@ def tile_list_kiln_burner_scores_kernel(
                         lhsT_scale=s[:, t * P : (t + 1) * P],
                         rhs=v_w[a][:, cols].bitcast(FP8X4),
                         rhs_scale=v_s[4 * a :, cols],
-                        start=(a == 0),
-                        stop=(a == 1),
+                        start=(a == 0 and t == 0),
+                        stop=(a == 1 and t == PACK - 1),
                     )
             r = factor[b, c]
-            tile = take(damped_turn)[:].rearrange("p (j t) -> p j t", t=PACK)
+            if tile is None:
+                tile = take(damped_turn)[:].rearrange("p (j t) -> p j t", t=PACK)
             nc.vector.tensor_tensor(
                 tile, acc.rearrange("p t j -> p j t"), r.rearrange("p (j t) -> p j t", t=PACK), ALU.mult
             )
@@ -275,40 +282,39 @@ def tile_list_kiln_burner_scores_kernel(
 
         keys = [[("w1", 0, b), ("w1", 1, b), ("ws", 0, b)] for b in range(BLOCKS)]
 
+        late_rooms = [raw[keys[1][1]][:, u * 2 * PASS : (u + 1) * 2 * PASS] for u in range(2)]
         magnitudes(0, 0)
-        squares(0, 0, 2)
+        squares(0, 0, 2, rooms[0][:])
         magnitudes(1, 0)
         factors(0, 0, 2)
         magnitudes(0, 1)
         magnitudes(1, 1)
         for key in keys[0]:
-            cast(key, nc.vector.tensor_copy)
+            cast(key, nc.vector.tensor_copy, take(grouped_turn)[:])
             quantize(key)
-        squares(0, 2, 2)
-        squares(0, 4, 2)
+        squares(0, 2, 2, rooms[1][:])
+        squares(0, 4, 2, rooms[0][:])
         factors(0, 2, 2)
-        squares(1, 0, 2)
         factors(0, 4, 2)
-        factors(1, 0, 2)
-        cast(keys[1][1], nc.scalar.copy)
-        squares(1, 2, 2)
-        cast(keys[1][2], nc.scalar.copy)
-        factors(1, 2, 2)
-        squares(1, 4, 2)
-        squares(0, 6, 2)
-        factors(1, 4, 2)
-        squares(1, 6, 2)
+        cast(keys[1][0], nc.scalar.copy, rooms[0][:].bitcast(BF16))
+        cast(keys[1][1], nc.scalar.copy, raw[keys[1][0]][:, : 2 * PASS].bitcast(BF16))
+        turns = list(late_rooms)
+        pieces = [(1, 0), (1, 2), (1, 4), (0, 6), (1, 6)]
+        squares(*pieces[0], 2, take(turns))
+        for k, (b, c0) in enumerate(pieces):
+            if k + 1 < len(pieces):
+                squares(*pieces[k + 1], 2, take(turns))
+            factors(b, c0, 2)
 
         order = [(0, c) for c in range(6)] + [(1, c) for c in range(6)] + [(0, 6), (0, 7), (1, 6), (1, 7)]
         damp(*order[0])
         for i, (b, c) in enumerate(order[:-2]):
             if (b, c) == (0, 2):
-                cast(keys[1][0], nc.vector.tensor_copy)
-            if (b, c) == (0, 3):
                 quantize(keys[1][0])
             if (b, c) == (0, 4):
                 quantize(keys[1][1])
             if (b, c) == (0, 5):
+                cast(keys[1][2], nc.vector.tensor_copy, factor_tile[0, 4][:].bitcast(BF16))
                 quantize(keys[1][2])
             damp(*order[i + 1])
             offset(b, c)
@@ -318,12 +324,10 @@ def tile_list_kiln_burner_scores_kernel(
                 quantize_h(0, 4, 2)
             if (b, c) == (1, 1):
                 quantize_h(1, 0, 2)
-                factors(0, 6, 2)
             if (b, c) == (1, 2):
                 scores(0, 2)
             if (b, c) == (1, 3):
                 quantize_h(1, 2, 2)
-                factors(1, 6, 2)
             if (b, c) == (1, 4):
                 scores(2, 2)
             if (b, c) == (1, 5):
@@ -332,7 +336,7 @@ def tile_list_kiln_burner_scores_kernel(
                 scores(4, 2)
         quantize_h(0, 6, 2)
         offset(1, 6)
-        damp(1, 7)
+        damp(1, 7, damped[1, 6])
         bank = take(e_turn)
         block_passes(bank, [0, 1, 2, 3], 0, 6)
         ends = [(take(a_turn), [0, 1]), (take(a_turn), [2, 3])]

@@ -19,10 +19,14 @@ ALU = mybir.AluOpType
 P = 128
 PACK = 4
 PASS = P * PACK
-HALF = 512
-CHUNK = 128
-BLOCKS = H // PASS
+BANK = 512
+HALF = S // 2
+CHUNK = BANK // PACK
+PAIR = 2
+LINE = 4
+BANDS = H // PASS
 CHUNKS = S // CHUNK
+LEAD = CHUNKS - PAIR
 
 
 def tile_list_kiln_burner_scores_kernel(
@@ -44,70 +48,70 @@ def tile_list_kiln_burner_scores_kernel(
         wd_s_raw = keep.tile([P, H], U8, name="wd_s_raw", align_bytes=64)
         wd_w = keep.tile([P, 2 * H], U8, name="wd_w", align_bytes=64)
         wd_s = keep.tile([P, H], U8, name="wd_s", align_bytes=64)
-        wo_w = keep.tile([P, 2, N], I32, name="wo_w", align_bytes=64)
+        wo_w = keep.tile([P, BANDS, N], I32, name="wo_w", align_bytes=64)
         wo_s = keep.tile([P, N], U8, name="wo_s", align_bytes=64)
-        bias = keep.tile([P, BLOCKS, PACK], F32, name="bias")
-        unit = keep.tile([P, 1], F32, name="unit")
+        bias = keep.tile([P, BANDS, PACK], F32, name="bias")
+        seed = keep.tile([P, 1], F32, name="seed")
         one = keep.tile([P, 1], F32, name="one")
 
-        def in_turn(pool, name, count, width, dtype):
-            return [pool.tile([P, width], dtype, name=f"{name}{k}", align_bytes=64) for k in range(count)]
-
-        banks = [psum.tile([P, HALF], F32, name=f"bank{k}") for k in range(8)]
-        a_turn, e_turn, s_turn = banks[0:3], banks[3:6], banks[6:8]
-        f_turn = [banks[6], banks[7], banks[5], banks[4]]
-        g_turn = in_turn(keep, "g", 4, PACK * HALF, F32)
-        grouped_turn = in_turn(keep, "grouped", 2, PACK * PASS, BF16)
-        rooms = in_turn(keep, "room", 2, PACK * 2 * CHUNK, F32)
-        damped_turn = in_turn(keep, "damped", 4, PACK * CHUNK, F32)
-        staged_turn = in_turn(keep, "staged", 4, HALF, F32)
+        def tiles(name, count, width, dtype):
+            return [keep.tile([P, width], dtype, name=f"{name}{k}", align_bytes=64) for k in range(count)]
 
         def take(turn):
             turn[:] = turn[1:] + turn[:1]
             return turn[-1]
 
+        banks = [psum.tile([P, BANK], F32, name=f"bank{k}") for k in range(8)]
+        a_turn, e_turn, score_turn = banks[0:3], banks[3:6], banks[6:8]
+        f_turn = [banks[6], banks[7], banks[5], banks[4]]
+        magnitude_turn = tiles("magnitude", BANDS * 2, PACK * HALF, F32)
+        grouped_turn = tiles("grouped", 2, PACK * PASS, BF16)
+        rooms = tiles("room", 2, PACK * PAIR * CHUNK, F32)
+        damped_turn = tiles("damped", 4, PACK * CHUNK, F32)
+        staged_turn = tiles("staged", 4, BANK, F32)
+
         nc.gpsimd.memset(wd_s_raw[:].bitcast(I32), 0)
         nc.vector.memset(xs_s[:].bitcast(I32), 0)
         nc.gpsimd.memset(tab_s[:].bitcast(I32), 0)
         nc.gpsimd.memset(wo_s[:].bitcast(I32), 0)
-        nc.vector.memset(unit[:], 1.0)
-        nc.scalar.activation(one[:], unit[:], ACT.Abs_reciprocal_sqrt)
+        nc.vector.memset(seed[:], 1.0)
+        nc.scalar.activation(one[:], seed[:], ACT.Abs_reciprocal_sqrt)
 
-        def load_planes(plane, scales, quadrants=range(4)):
+        def load_scales(tile, scales, quadrants=range(4)):
             rows = 4 * scales.shape[0]
             for q in quadrants:
                 nc.sync.dma_start(
-                    plane[32 * q : 32 * q + rows, :].bitcast(I32), scales[:, 4 * q : 4 * q + 4, :].bitcast(I32)
+                    tile[32 * q : 32 * q + rows, :].bitcast(I32), scales[:, 4 * q : 4 * q + 4, :].bitcast(I32)
                 )
 
         def words(dram):
             return dram.rearrange("p n t -> p (n t)").bitcast(I32)
 
-        load_planes(wd_s_raw, wd_scales)
-        load_planes(xs_s, xs_scales, range(2))
+        load_scales(wd_s_raw, wd_scales)
+        load_scales(xs_s, xs_scales, range(2))
         nc.sync.dma_start(wd_w_raw[:].bitcast(I32), wd_words[0].bitcast(I32))
         nc.sync.dma_start(xs_w[0][:], words(xs_words[0])[:, :HALF])
-        load_planes(xs_s, xs_scales, range(2, 4))
+        load_scales(xs_s, xs_scales, range(2, 4))
         nc.sync.dma_start(bias[:], bd.rearrange("(b p t) -> p b t", p=P, t=PACK))
         nc.sync.dma_start(xs_w[1][:], words(xs_words[0])[:, HALF:])
         nc.sync.dma_start(offsets[:], offs)
-        load_planes(tab_s, tab_scales)
+        load_scales(tab_s, tab_scales)
         for a in range(2):
             nc.sync.dma_start(tab_w[a][:], words(tab_words[a]))
 
         raw = {}
-        for b in range(BLOCKS):
-            for name, w, a in (("w1", w1, 0), ("w1", w1, 1), ("ws", ws, 0)):
+        for b in range(BANDS):
+            for name, weight, a in (("w1", w1, 0), ("w1", w1, 1), ("ws", ws, 0)):
                 tile = keep.tile([P, PACK * PASS], F32, name=f"raw_{name}_{a}_{b}", align_bytes=64)
-                rows = w[a * PASS : (a + 1) * PASS, b * PASS : (b + 1) * PASS]
+                rows = weight[a * PASS : (a + 1) * PASS, b * PASS : (b + 1) * PASS]
                 nc.sync.dma_start(
-                    tile[:].rearrange("p (j c) -> p j c", j=PACK), rows.rearrange("(p j) c -> p j c", j=PACK)
+                    tile[:].rearrange("p (i c) -> p i c", i=PACK), rows.rearrange("(p i) c -> p i c", i=PACK)
                 )
                 raw[name, a, b] = tile
         nc.sync.dma_start(wo_w[:], wo_words.rearrange("a p n t -> p a (n t)").bitcast(I32))
-        load_planes(wo_s, wo_scales)
+        load_scales(wo_s, wo_scales)
 
-        for b in range(BLOCKS):
+        for b in range(BANDS):
             for dst, src in ((wd_w[:].bitcast(U16), wd_w_raw[:].bitcast(U16)), (wd_s[:], wd_s_raw[:])):
                 nc.vector.tensor_copy(
                     dst.rearrange("p (t c) -> p c t", t=PACK)[:, b * P : (b + 1) * P, :],
@@ -118,78 +122,64 @@ def tile_list_kiln_burner_scores_kernel(
         for a in range(2):
             nc.vector.tensor_copy(v_w[a][:], tab_w[a][:].bitcast(U32).indirect(offsets[:]))
 
-        magnitude = {}
-        factor = {}
-        factor_tile = {}
-        squared = {}
+        magnitude, root, factor = {}, {}, {}
+        grouped, codes, damped = {}, {}, {}
 
         def magnitudes(b, half):
-            cols = slice(half * HALF, (half + 1) * HALF)
-            g = take(g_turn)[:].rearrange("p (t j) -> p t j", t=PACK)
+            tile = take(magnitude_turn)[:].rearrange("p (t j) -> p t j", t=PACK)
             for t in range(PACK):
                 first = t * (H // PACK) + b * P
-                f = take(f_turn)
+                acc = take(f_turn)
                 nc.tensor.matmul_mx(
-                    f[:],
+                    acc[:],
                     lhsT=wd_w[:, 2 * first : 2 * (first + P)].bitcast(FP4X4),
                     lhsT_scale=wd_s[:, first : first + P],
                     rhs=xs_w[half][:].bitcast(FP8X4),
-                    rhs_scale=xs_s[:, cols],
+                    rhs_scale=xs_s[:, half * HALF : (half + 1) * HALF],
                     start=True,
                     stop=True,
                 )
-                nc.scalar.activation(g[:, t, :], f[:], ACT.Abs, bias=bias[:, b, t : t + 1])
-            magnitude[b, half] = g
+                nc.scalar.activation(tile[:, t, :], acc[:], ACT.Abs, bias=bias[:, b, t : t + 1])
+            magnitude[b, half] = tile
 
-        def piece(b, c0, count):
-            half, inside = divmod(c0 * CHUNK, HALF)
-            return magnitude[b, half][:, :, inside : inside + count * CHUNK]
+        def roots(b, c, room):
+            half, inside = divmod(c * CHUNK, HALF)
+            root[b, c] = room.rearrange("p (t j) -> p t j", t=PACK)
+            source = magnitude[b, half][:, :, inside : inside + PAIR * CHUNK]
+            nc.scalar.activation(root[b, c], source, ACT.Abs_reciprocal_sqrt, bias=one[:])
 
-        def squares(b, c0, count, room):
-            square = room.rearrange("p (t j) -> p t j", t=PACK)
-            nc.scalar.activation(square, piece(b, c0, count), ACT.Square, bias=one[:])
-            squared[b, c0] = square
-
-        def factors(b, c0, count):
-            g = squared[b, c0]
-            r = keep.tile([P, count * CHUNK * PACK], F32, name=f"r_{b}_{c0}", align_bytes=64)
-            factor_tile[b, c0] = r
+        def factors(b, c):
+            factor[b, c] = keep.tile([P, PAIR * CHUNK * PACK], F32, name=f"factor_{b}_{c}", align_bytes=64)
             nc.scalar.activation(
-                r[:].rearrange("p (c i t) -> p c t i", i=4, t=PACK),
-                g.rearrange("p t (c i) -> p c t i", i=4),
-                ACT.Abs_reciprocal_sqrt,
+                factor[b, c][:].rearrange("p (u i t) -> p u t i", i=LINE, t=PACK),
+                root[b, c].rearrange("p t (u i) -> p u t i", i=LINE),
+                ACT.Square,
             )
-            for k in range(count):
-                factor[b, c0 + k] = r[:, k * CHUNK * PACK : (k + 1) * CHUNK * PACK]
 
-        grouped = {}
-        codes = {}
-
-        def cast(key, copy, tile):
+        def cast(key, copy, room):
             copy(
-                tile.rearrange("p (t m j) -> p m j t", t=PACK, j=PACK),
-                raw[key][:].rearrange("p (j m t) -> p m j t", j=PACK, t=PACK),
+                room.rearrange("p (t m i) -> p m i t", t=PACK, i=PACK),
+                raw[key][:].rearrange("p (i m t) -> p m i t", i=PACK, t=PACK),
             )
-            grouped[key] = tile
+            grouped[key] = room
 
-        def quantize(key):
+        def quantize_weight(key):
             name, a, b = key
-            w = keep.tile([P, PASS], U32, name=f"q_{name}_{a}_{b}", align_bytes=64)
-            s = keep.tile([P, PASS], U8, name=f"s_{name}_{a}_{b}", align_bytes=64)
+            w = keep.tile([P, PASS], U32, name=f"codes_{name}_{a}_{b}", align_bytes=64)
+            s = keep.tile([P, PASS], U8, name=f"scales_{name}_{a}_{b}", align_bytes=64)
             nc.vector.quantize_mx(w[:].bitcast(FP8X4), s[:], grouped[key])
             codes[key] = (w, s)
 
-        h = [keep.tile([P, S * PACK], BF16, name=f"h{b}", align_bytes=64) for b in range(BLOCKS)]
-        h_w = [keep.tile([P, S], U32, name=f"h_w{b}", align_bytes=64) for b in range(BLOCKS)]
-        h_s = [keep.tile([P, S], U8, name=f"h_s{b}", align_bytes=64) for b in range(BLOCKS)]
-        damped = {}
+        h = tiles("h", BANDS, S * PACK, BF16)
+        h_w = tiles("h_w", BANDS, S, U32)
+        h_s = tiles("h_s", BANDS, S, U8)
 
-        def damp(b, c, tile=None):
+        def damp(b, c, room):
             cols = slice(c * CHUNK, (c + 1) * CHUNK)
             acc = take(a_turn)[:].rearrange("p (t j) -> p t j", t=PACK)
             for a in range(2):
+                w, s = codes["w1", a, b]
                 for t in range(PACK):
-                    w, s = codes["w1", a, b]
                     nc.tensor.matmul_mx(
                         acc[:, t, :],
                         lhsT=w[:, t * P : (t + 1) * P].bitcast(FP8X4),
@@ -199,16 +189,17 @@ def tile_list_kiln_burner_scores_kernel(
                         start=(a == 0 and t == 0),
                         stop=(a == 1 and t == PACK - 1),
                     )
-            r = factor[b, c]
-            if tile is None:
-                tile = take(damped_turn)[:].rearrange("p (j t) -> p j t", t=PACK)
+            inside = c % PAIR
+            r = factor[b, c - inside][:, inside * BANK : (inside + 1) * BANK]
+            damped[b, c] = room
             nc.vector.tensor_tensor(
-                tile, acc.rearrange("p t j -> p j t"), r.rearrange("p (j t) -> p j t", t=PACK), ALU.mult
+                room[:].rearrange("p (j t) -> p j t", t=PACK),
+                acc.rearrange("p t j -> p j t"),
+                r.rearrange("p (j t) -> p j t", t=PACK),
+                ALU.mult,
             )
-            damped[b, c] = tile
 
-        def offset(b, c):
-            cols = slice(c * CHUNK, (c + 1) * CHUNK)
+        def subtract(b, c):
             acc = take(e_turn)[:].rearrange("p (t j) -> p t j", t=PACK)
             w, s = codes["ws", 0, b]
             half, inside = divmod(c * CHUNK, HALF)
@@ -218,20 +209,19 @@ def tile_list_kiln_burner_scores_kernel(
                     lhsT=w[:, t * P : (t + 1) * P].bitcast(FP8X4),
                     lhsT_scale=s[:, t * P : (t + 1) * P],
                     rhs=xs_w[half][:, inside : inside + CHUNK].bitcast(FP8X4),
-                    rhs_scale=xs_s[:, cols],
+                    rhs_scale=xs_s[:, c * CHUNK : (c + 1) * CHUNK],
                     start=True,
                     stop=True,
                 )
-            dst = h[b][:, c * CHUNK * PACK : (c + 1) * CHUNK * PACK]
             nc.vector.tensor_tensor(
-                dst.rearrange("p (j t) -> p j t", t=PACK),
-                damped[b, c],
+                h[b][:, c * BANK : (c + 1) * BANK].rearrange("p (j t) -> p j t", t=PACK),
+                damped[b, c][:].rearrange("p (j t) -> p j t", t=PACK),
                 acc.rearrange("p t j -> p j t"),
                 ALU.subtract,
             )
 
-        def quantize_h(b, c0, count):
-            first, last = c0 * CHUNK, (c0 + count) * CHUNK
+        def quantize_h(b, c, count):
+            first, last = c * CHUNK, (c + count) * CHUNK
             nc.vector.quantize_mx(
                 h_w[b][:, first:last].bitcast(FP8X4), h_s[b][:, first:last], h[b][:, first * PACK : last * PACK]
             )
@@ -249,105 +239,101 @@ def tile_list_kiln_burner_scores_kernel(
                 stop=stop,
             )
 
-        def scores(c0, count):
-            width = count * CHUNK
-            cols = slice(c0 * CHUNK, c0 * CHUNK + width)
-            per_bank = HALF // width
-            for n0 in range(0, N // P, per_bank):
-                acc = take(s_turn)
-                for k in range(per_bank):
-                    for b in range(BLOCKS):
-                        score_pass(acc[:, k * width : (k + 1) * width], n0 + k, b, cols, b == 0, b == BLOCKS - 1)
-                tile = take(staged_turn)
-                nc.scalar.copy(tile[:], acc[:])
-                nc.sync.dma_start(
-                    out_rows[:, n0 : n0 + per_bank, cols], tile[:].rearrange("p (n j) -> p n j", n=per_bank)
-                )
-
-        def block_passes(acc, tiles, b, c):
-            cols = slice(c * CHUNK, (c + 1) * CHUNK)
-            for k, n in enumerate(tiles):
-                first = b == 0 and k == 0
-                final = b == BLOCKS - 1 and k == len(tiles) - 1
-                score_pass(acc[:, k * CHUNK : (k + 1) * CHUNK], n, b, cols, first, final)
-
-        def store(acc, tiles, c, copy, queue):
-            width = len(tiles) * CHUNK
-            tile = take(staged_turn)[:, :width]
-            copy(tile, acc[:, :width])
+        def store(bank, row_tiles, cols, copy, queue):
+            width = len(row_tiles) * (cols.stop - cols.start)
+            staged = take(staged_turn)[:, :width]
+            copy(staged, bank[:, :width])
             queue.dma_start(
-                out_rows[:, tiles[0] : tiles[-1] + 1, c * CHUNK : (c + 1) * CHUNK],
-                tile.rearrange("p (n j) -> p n j", j=CHUNK),
+                out_rows[:, row_tiles.start : row_tiles.stop, cols],
+                staged.rearrange("p (n j) -> p n j", n=len(row_tiles)),
             )
 
-        keys = [[("w1", 0, b), ("w1", 1, b), ("ws", 0, b)] for b in range(BLOCKS)]
+        def pair_scores(c):
+            width = PAIR * CHUNK
+            cols = slice(c * CHUNK, c * CHUNK + width)
+            for n0 in range(0, N // P, BANK // width):
+                row_tiles = range(n0, n0 + BANK // width)
+                bank = take(score_turn)
+                for k, n in enumerate(row_tiles):
+                    for b in range(BANDS):
+                        score_pass(bank[:, k * width : (k + 1) * width], n, b, cols, b == 0, b == BANDS - 1)
+                store(bank, row_tiles, cols, nc.scalar.copy, nc.sync)
 
-        late_rooms = [raw[keys[1][1]][:, u * 2 * PASS : (u + 1) * 2 * PASS] for u in range(2)]
+        def band_scores(bank, row_tiles, b, cols):
+            for k, n in enumerate(row_tiles):
+                start = b == 0 and k == 0
+                stop = b == BANDS - 1 and k == len(row_tiles) - 1
+                score_pass(bank[:, k * CHUNK : (k + 1) * CHUNK], n, b, cols, start, stop)
+
+        early, late = [[("w1", 0, b), ("w1", 1, b), ("ws", 0, b)] for b in range(BANDS)]
+        room_words = PACK * PAIR * CHUNK
+
         magnitudes(0, 0)
-        squares(0, 0, 2, rooms[0][:])
+        roots(0, 0, rooms[0][:])
         magnitudes(1, 0)
-        factors(0, 0, 2)
+        factors(0, 0)
         magnitudes(0, 1)
         magnitudes(1, 1)
-        for key in keys[0]:
+        for key in early:
             cast(key, nc.vector.tensor_copy, take(grouped_turn)[:])
-            quantize(key)
-        squares(0, 2, 2, rooms[1][:])
-        squares(0, 4, 2, rooms[0][:])
-        factors(0, 2, 2)
-        factors(0, 4, 2)
-        cast(keys[1][0], nc.scalar.copy, rooms[0][:].bitcast(BF16))
-        cast(keys[1][1], nc.scalar.copy, raw[keys[1][0]][:, : 2 * PASS].bitcast(BF16))
-        turns = list(late_rooms)
-        pieces = [(1, 0), (1, 2), (1, 4), (0, 6), (1, 6)]
-        squares(*pieces[0], 2, take(turns))
-        for k, (b, c0) in enumerate(pieces):
-            if k + 1 < len(pieces):
-                squares(*pieces[k + 1], 2, take(turns))
-            factors(b, c0, 2)
+            quantize_weight(key)
 
-        order = [(0, c) for c in range(6)] + [(1, c) for c in range(6)] + [(0, 6), (0, 7), (1, 6), (1, 7)]
-        damp(*order[0])
-        for i, (b, c) in enumerate(order[:-2]):
-            if (b, c) == (0, 2):
-                quantize(keys[1][0])
-            if (b, c) == (0, 4):
-                quantize(keys[1][1])
-            if (b, c) == (0, 5):
-                cast(keys[1][2], nc.vector.tensor_copy, factor_tile[0, 4][:].bitcast(BF16))
-                quantize(keys[1][2])
-            damp(*order[i + 1])
-            offset(b, c)
-            if (b, c) == (0, 3):
-                quantize_h(0, 0, 4)
-            if (b, c) == (0, 5):
-                quantize_h(0, 4, 2)
-            if (b, c) == (1, 1):
-                quantize_h(1, 0, 2)
-            if (b, c) == (1, 2):
-                scores(0, 2)
-            if (b, c) == (1, 3):
-                quantize_h(1, 2, 2)
-            if (b, c) == (1, 4):
-                scores(2, 2)
-            if (b, c) == (1, 5):
-                quantize_h(1, 4, 2)
-            if (b, c) == (0, 6):
-                scores(4, 2)
-        quantize_h(0, 6, 2)
-        offset(1, 6)
-        damp(1, 7, damped[1, 6])
-        bank = take(e_turn)
-        block_passes(bank, [0, 1, 2, 3], 0, 6)
-        ends = [(take(a_turn), [0, 1]), (take(a_turn), [2, 3])]
-        for acc, tiles in ends:
-            block_passes(acc, tiles, 0, 7)
-        quantize_h(1, 6, 1)
-        block_passes(bank, [0, 1, 2, 3], 1, 6)
-        store(bank, [0, 1, 2, 3], 6, nc.scalar.copy, nc.sync)
-        offset(1, 7)
-        quantize_h(1, 7, 1)
-        for acc, tiles in ends:
-            block_passes(acc, tiles, 1, 7)
-        store(*ends[0], 7, nc.vector.tensor_copy, nc.sync)
-        store(*ends[1], 7, nc.scalar.copy, nc.scalar)
+        roots(0, PAIR, rooms[1][:])
+        roots(0, 2 * PAIR, rooms[0][:])
+        factors(0, PAIR)
+        factors(0, 2 * PAIR)
+        cast(late[0], nc.scalar.copy, rooms[0][:].bitcast(BF16))
+        cast(late[1], nc.scalar.copy, raw[late[0]][:, :room_words].bitcast(BF16))
+
+        steps = [(b, c) for b in range(BANDS) for c in range(LEAD)]
+        steps = steps + [(b, c) for b in range(BANDS) for c in range(LEAD, CHUNKS)]
+        pairs = [(b, c) for b, c in steps[LEAD:] if c % PAIR == 0]
+        late_rooms = [raw[late[1]][:, u * room_words : (u + 1) * room_words] for u in range(2)]
+        roots(*pairs[0], take(late_rooms))
+        for k, pair in enumerate(pairs):
+            if k + 1 < len(pairs):
+                roots(*pairs[k + 1], take(late_rooms))
+            factors(*pair)
+
+        damp(*steps[0], take(damped_turn))
+        scores_due = []
+        for i, (b, c) in enumerate(steps[:-PAIR]):
+            if i == LEAD - 2 * PAIR:
+                quantize_weight(late[0])
+            if i == LEAD - PAIR:
+                quantize_weight(late[1])
+            if i == LEAD - 1:
+                cast(late[2], nc.vector.tensor_copy, factor[0, LEAD - PAIR][:].bitcast(BF16))
+                quantize_weight(late[2])
+            damp(*steps[i + 1], take(damped_turn))
+            subtract(b, c)
+            for first in scores_due:
+                pair_scores(first)
+            scores_due = []
+            if (b, c) == (0, 2 * PAIR - 1):
+                quantize_h(b, 0, 2 * PAIR)
+            elif c % PAIR == PAIR - 1 and (b, c) > (0, 2 * PAIR):
+                quantize_h(b, c + 1 - PAIR, PAIR)
+                if b == BANDS - 1:
+                    scores_due = [c + 1 - PAIR]
+
+        b, before, last = BANDS - 1, CHUNKS - 2, CHUNKS - 1
+        before_cols = slice(before * CHUNK, last * CHUNK)
+        last_cols = slice(last * CHUNK, S)
+        all_rows = range(N // P)
+        subtract(b, before)
+        damp(b, last, damped[b, before])
+        before_bank = take(e_turn)
+        band_scores(before_bank, all_rows, 0, before_cols)
+        ends = [(take(a_turn), range(0, 2)), (take(a_turn), range(2, 4))]
+        for bank, row_tiles in ends:
+            band_scores(bank, row_tiles, 0, last_cols)
+        quantize_h(b, before, 1)
+        band_scores(before_bank, all_rows, b, before_cols)
+        store(before_bank, all_rows, before_cols, nc.scalar.copy, nc.sync)
+        subtract(b, last)
+        quantize_h(b, last, 1)
+        for bank, row_tiles in ends:
+            band_scores(bank, row_tiles, b, last_cols)
+        store(*ends[0], last_cols, nc.vector.tensor_copy, nc.sync)
+        store(*ends[1], last_cols, nc.scalar.copy, nc.scalar)

from contextlib import ExitStack

import concourse.mybir as mybir

K, K2, H, N, T, S = 1024, 512, 1024, 512, 2048, 1024
FLOPS = 2 * S * (K * H + 2 * K2 * H + H * N)

F32 = mybir.dt.float32
BF16 = mybir.dt.bfloat16
I32 = mybir.dt.int32
U32 = mybir.dt.uint32
U16 = mybir.dt.uint16
U8 = mybir.dt.uint8
FP8X4 = mybir.dt.float8_e4m3fn_x4
FP4X4 = mybir.dt.float4_e2m1fn_x4
ACT = mybir.ActivationFunctionType
ALU = mybir.AluOpType

P = 128
PACK = 4
PASS = P * PACK
BANK = 512
HALF = S // 2
CHUNK = BANK // PACK
PAIR = 2
LINE = 4
BANDS = H // PASS
CHUNKS = S // CHUNK
LEAD = CHUNKS - PAIR


def tile_list_kiln_burner_scores_kernel(
    tc, tab_words, tab_scales, offs, xs_words, xs_scales, w1, wd_words, wd_scales, bd, ws, wo_words, wo_scales, out
):
    nc = tc.nc
    with ExitStack() as ctx:
        keep = ctx.enter_context(tc.tile_pool(name="keep", bufs=1))
        psum = ctx.enter_context(tc.psum_pool(name="psum", bufs=1))

        offsets = keep.tile([P, S // 16], U16, name="offsets")
        tab_w = [keep.tile([P, T], I32, name=f"tab_w{a}", align_bytes=64) for a in range(2)]
        tab_s = keep.tile([P, T], U8, name="tab_s", align_bytes=64)
        v_w = [keep.tile([P, S], U32, name=f"v_w{a}", align_bytes=64) for a in range(2)]
        v_s = keep.tile([P, S], U8, name="v_s", align_bytes=64)
        xs_w = [keep.tile([P, HALF], I32, name=f"xs_w{half}", align_bytes=64) for half in range(2)]
        xs_s = keep.tile([P, S], U8, name="xs_s", align_bytes=64)
        wd_w_raw = keep.tile([P, 2 * H], U8, name="wd_w_raw", align_bytes=64)
        wd_s_raw = keep.tile([P, H], U8, name="wd_s_raw", align_bytes=64)
        wd_w = keep.tile([P, 2 * H], U8, name="wd_w", align_bytes=64)
        wd_s = keep.tile([P, H], U8, name="wd_s", align_bytes=64)
        wo_w = keep.tile([P, BANDS, N], I32, name="wo_w", align_bytes=64)
        wo_s = keep.tile([P, N], U8, name="wo_s", align_bytes=64)
        bias = keep.tile([P, BANDS, PACK], F32, name="bias")
        seed = keep.tile([P, 1], F32, name="seed")
        one = keep.tile([P, 1], F32, name="one")

        def tiles(name, count, width, dtype):
            return [keep.tile([P, width], dtype, name=f"{name}{k}", align_bytes=64) for k in range(count)]

        def take(turn):
            turn[:] = turn[1:] + turn[:1]
            return turn[-1]

        banks = [psum.tile([P, BANK], F32, name=f"bank{k}") for k in range(8)]
        a_turn, e_turn, score_turn = banks[0:3], banks[3:6], banks[6:8]
        f_turn = [banks[6], banks[7], banks[5], banks[4]]
        magnitude_turn = tiles("magnitude", BANDS * 2, PACK * HALF, F32)
        grouped_turn = tiles("grouped", 2, PACK * PASS, BF16)
        rooms = tiles("room", 2, PACK * PAIR * CHUNK, F32)
        damped_turn = tiles("damped", 4, PACK * CHUNK, F32)
        staged_turn = tiles("staged", 4, BANK, F32)

        nc.gpsimd.memset(wd_s_raw[:].bitcast(I32), 0)
        nc.vector.memset(xs_s[:].bitcast(I32), 0)
        nc.gpsimd.memset(tab_s[:].bitcast(I32), 0)
        nc.gpsimd.memset(wo_s[:].bitcast(I32), 0)
        nc.vector.memset(seed[:], 1.0)
        nc.scalar.activation(one[:], seed[:], ACT.Abs_reciprocal_sqrt)

        def load_scales(tile, scales, quadrants=range(4)):
            rows = 4 * scales.shape[0]
            for q in quadrants:
                nc.sync.dma_start(
                    tile[32 * q : 32 * q + rows, :].bitcast(I32), scales[:, 4 * q : 4 * q + 4, :].bitcast(I32)
                )

        def words(dram):
            return dram.rearrange("p n t -> p (n t)").bitcast(I32)

        load_scales(wd_s_raw, wd_scales)
        load_scales(xs_s, xs_scales, range(2))
        nc.sync.dma_start(wd_w_raw[:].bitcast(I32), wd_words[0].bitcast(I32))
        nc.sync.dma_start(xs_w[0][:], words(xs_words[0])[:, :HALF])
        load_scales(xs_s, xs_scales, range(2, 4))
        nc.sync.dma_start(bias[:], bd.rearrange("(b p t) -> p b t", p=P, t=PACK))
        nc.sync.dma_start(xs_w[1][:], words(xs_words[0])[:, HALF:])
        nc.sync.dma_start(offsets[:], offs)
        load_scales(tab_s, tab_scales)
        for a in range(2):
            nc.sync.dma_start(tab_w[a][:], words(tab_words[a]))

        raw = {}
        for b in range(BANDS):
            for name, weight, a in (("w1", w1, 0), ("w1", w1, 1), ("ws", ws, 0)):
                tile = keep.tile([P, PACK * PASS], F32, name=f"raw_{name}_{a}_{b}", align_bytes=64)
                rows = weight[a * PASS : (a + 1) * PASS, b * PASS : (b + 1) * PASS]
                nc.sync.dma_start(
                    tile[:].rearrange("p (i c) -> p i c", i=PACK), rows.rearrange("(p i) c -> p i c", i=PACK)
                )
                raw[name, a, b] = tile
        nc.sync.dma_start(wo_w[:], wo_words.rearrange("a p n t -> p a (n t)").bitcast(I32))
        load_scales(wo_s, wo_scales)

        for b in range(BANDS):
            for dst, src in ((wd_w[:].bitcast(U16), wd_w_raw[:].bitcast(U16)), (wd_s[:], wd_s_raw[:])):
                nc.vector.tensor_copy(
                    dst.rearrange("p (t c) -> p c t", t=PACK)[:, b * P : (b + 1) * P, :],
                    src.rearrange("p (c t) -> p c t", t=PACK)[:, b * P : (b + 1) * P, :],
                )

        nc.vector.tensor_copy(v_s[:], tab_s[:].indirect(offsets[:]))
        for a in range(2):
            nc.vector.tensor_copy(v_w[a][:], tab_w[a][:].bitcast(U32).indirect(offsets[:]))

        magnitude, root, factor = {}, {}, {}
        grouped, codes, damped = {}, {}, {}

        def magnitudes(b, half):
            tile = take(magnitude_turn)[:].rearrange("p (t j) -> p t j", t=PACK)
            for t in range(PACK):
                first = t * (H // PACK) + b * P
                acc = take(f_turn)
                nc.tensor.matmul_mx(
                    acc[:],
                    lhsT=wd_w[:, 2 * first : 2 * (first + P)].bitcast(FP4X4),
                    lhsT_scale=wd_s[:, first : first + P],
                    rhs=xs_w[half][:].bitcast(FP8X4),
                    rhs_scale=xs_s[:, half * HALF : (half + 1) * HALF],
                    start=True,
                    stop=True,
                )
                nc.scalar.activation(tile[:, t, :], acc[:], ACT.Abs, bias=bias[:, b, t : t + 1])
            magnitude[b, half] = tile

        def roots(b, c, room):
            half, inside = divmod(c * CHUNK, HALF)
            root[b, c] = room.rearrange("p (t j) -> p t j", t=PACK)
            source = magnitude[b, half][:, :, inside : inside + PAIR * CHUNK]
            nc.scalar.activation(root[b, c], source, ACT.Abs_reciprocal_sqrt, bias=one[:])

        def factors(b, c):
            factor[b, c] = keep.tile([P, PAIR * CHUNK * PACK], F32, name=f"factor_{b}_{c}", align_bytes=64)
            nc.scalar.activation(
                factor[b, c][:].rearrange("p (u i t) -> p u t i", i=LINE, t=PACK),
                root[b, c].rearrange("p t (u i) -> p u t i", i=LINE),
                ACT.Square,
            )

        def cast(key, copy, room):
            copy(
                room.rearrange("p (t m i) -> p m i t", t=PACK, i=PACK),
                raw[key][:].rearrange("p (i m t) -> p m i t", i=PACK, t=PACK),
            )
            grouped[key] = room

        def quantize_weight(key):
            name, a, b = key
            w = keep.tile([P, PASS], U32, name=f"codes_{name}_{a}_{b}", align_bytes=64)
            s = keep.tile([P, PASS], U8, name=f"scales_{name}_{a}_{b}", align_bytes=64)
            nc.vector.quantize_mx(w[:].bitcast(FP8X4), s[:], grouped[key])
            codes[key] = (w, s)

        h = tiles("h", BANDS, S * PACK, BF16)
        h_w = tiles("h_w", BANDS, S, U32)
        h_s = tiles("h_s", BANDS, S, U8)

        def damp(b, c, room):
            cols = slice(c * CHUNK, (c + 1) * CHUNK)
            acc = take(a_turn)[:].rearrange("p (t j) -> p t j", t=PACK)
            for a in range(2):
                w, s = codes["w1", a, b]
                for t in range(PACK):
                    nc.tensor.matmul_mx(
                        acc[:, t, :],
                        lhsT=w[:, t * P : (t + 1) * P].bitcast(FP8X4),
                        lhsT_scale=s[:, t * P : (t + 1) * P],
                        rhs=v_w[a][:, cols].bitcast(FP8X4),
                        rhs_scale=v_s[4 * a :, cols],
                        start=(a == 0 and t == 0),
                        stop=(a == 1 and t == PACK - 1),
                    )
            inside = c % PAIR
            r = factor[b, c - inside][:, inside * BANK : (inside + 1) * BANK]
            damped[b, c] = room
            nc.vector.tensor_tensor(
                room[:].rearrange("p (j t) -> p j t", t=PACK),
                acc.rearrange("p t j -> p j t"),
                r.rearrange("p (j t) -> p j t", t=PACK),
                ALU.mult,
            )

        def subtract(b, c):
            acc = take(e_turn)[:].rearrange("p (t j) -> p t j", t=PACK)
            w, s = codes["ws", 0, b]
            half, inside = divmod(c * CHUNK, HALF)
            for t in range(PACK):
                nc.tensor.matmul_mx(
                    acc[:, t, :],
                    lhsT=w[:, t * P : (t + 1) * P].bitcast(FP8X4),
                    lhsT_scale=s[:, t * P : (t + 1) * P],
                    rhs=xs_w[half][:, inside : inside + CHUNK].bitcast(FP8X4),
                    rhs_scale=xs_s[:, c * CHUNK : (c + 1) * CHUNK],
                    start=True,
                    stop=True,
                )
            nc.vector.tensor_tensor(
                h[b][:, c * BANK : (c + 1) * BANK].rearrange("p (j t) -> p j t", t=PACK),
                damped[b, c][:].rearrange("p (j t) -> p j t", t=PACK),
                acc.rearrange("p t j -> p j t"),
                ALU.subtract,
            )

        def quantize_h(b, c, count):
            first, last = c * CHUNK, (c + count) * CHUNK
            nc.vector.quantize_mx(
                h_w[b][:, first:last].bitcast(FP8X4), h_s[b][:, first:last], h[b][:, first * PACK : last * PACK]
            )

        out_rows = out.rearrange("(n p) j -> p n j", p=P)

        def score_pass(acc, n, b, cols, start, stop):
            nc.tensor.matmul_mx(
                acc,
                lhsT=wo_w[:, b, n * P : (n + 1) * P].bitcast(FP8X4),
                lhsT_scale=wo_s[4 * b :, n * P : (n + 1) * P],
                rhs=h_w[b][:, cols].bitcast(FP8X4),
                rhs_scale=h_s[b][:, cols],
                start=start,
                stop=stop,
            )

        def store(bank, row_tiles, cols, copy, queue):
            width = len(row_tiles) * (cols.stop - cols.start)
            staged = take(staged_turn)[:, :width]
            copy(staged, bank[:, :width])
            queue.dma_start(
                out_rows[:, row_tiles.start : row_tiles.stop, cols],
                staged.rearrange("p (n j) -> p n j", n=len(row_tiles)),
            )

        def pair_scores(c):
            width = PAIR * CHUNK
            cols = slice(c * CHUNK, c * CHUNK + width)
            for n0 in range(0, N // P, BANK // width):
                row_tiles = range(n0, n0 + BANK // width)
                bank = take(score_turn)
                for k, n in enumerate(row_tiles):
                    for b in range(BANDS):
                        score_pass(bank[:, k * width : (k + 1) * width], n, b, cols, b == 0, b == BANDS - 1)
                store(bank, row_tiles, cols, nc.scalar.copy, nc.sync)

        def band_scores(bank, row_tiles, b, cols):
            for k, n in enumerate(row_tiles):
                start = b == 0 and k == 0
                stop = b == BANDS - 1 and k == len(row_tiles) - 1
                score_pass(bank[:, k * CHUNK : (k + 1) * CHUNK], n, b, cols, start, stop)

        early, late = [[("w1", 0, b), ("w1", 1, b), ("ws", 0, b)] for b in range(BANDS)]
        room_words = PACK * PAIR * CHUNK

        magnitudes(0, 0)
        roots(0, 0, rooms[0][:])
        magnitudes(1, 0)
        factors(0, 0)
        magnitudes(0, 1)
        magnitudes(1, 1)
        for key in early:
            cast(key, nc.vector.tensor_copy, take(grouped_turn)[:])
            quantize_weight(key)

        roots(0, PAIR, rooms[1][:])
        roots(0, 2 * PAIR, rooms[0][:])
        factors(0, PAIR)
        factors(0, 2 * PAIR)
        cast(late[0], nc.scalar.copy, rooms[0][:].bitcast(BF16))
        cast(late[1], nc.scalar.copy, raw[late[0]][:, :room_words].bitcast(BF16))

        steps = [(b, c) for b in range(BANDS) for c in range(LEAD)]
        steps = steps + [(b, c) for b in range(BANDS) for c in range(LEAD, CHUNKS)]
        pairs = [(b, c) for b, c in steps[LEAD:] if c % PAIR == 0]
        late_rooms = [raw[late[1]][:, u * room_words : (u + 1) * room_words] for u in range(2)]
        roots(*pairs[0], take(late_rooms))
        for k, pair in enumerate(pairs):
            if k + 1 < len(pairs):
                roots(*pairs[k + 1], take(late_rooms))
            factors(*pair)

        damp(*steps[0], take(damped_turn))
        scores_due = []
        for i, (b, c) in enumerate(steps[:-PAIR]):
            if i == LEAD - 2 * PAIR:
                quantize_weight(late[0])
            if i == LEAD - PAIR:
                quantize_weight(late[1])
            if i == LEAD - 1:
                cast(late[2], nc.vector.tensor_copy, factor[0, LEAD - PAIR][:].bitcast(BF16))
                quantize_weight(late[2])
            damp(*steps[i + 1], take(damped_turn))
            subtract(b, c)
            for first in scores_due:
                pair_scores(first)
            scores_due = []
            if (b, c) == (0, 2 * PAIR - 1):
                quantize_h(b, 0, 2 * PAIR)
            elif c % PAIR == PAIR - 1 and (b, c) > (0, 2 * PAIR):
                quantize_h(b, c + 1 - PAIR, PAIR)
                if b == BANDS - 1:
                    scores_due = [c + 1 - PAIR]

        b, before, last = BANDS - 1, CHUNKS - 2, CHUNKS - 1
        before_cols = slice(before * CHUNK, last * CHUNK)
        last_cols = slice(last * CHUNK, S)
        all_rows = range(N // P)
        subtract(b, before)
        damp(b, last, damped[b, before])
        before_bank = take(e_turn)
        band_scores(before_bank, all_rows, 0, before_cols)
        ends = [(take(a_turn), range(0, 2)), (take(a_turn), range(2, 4))]
        for bank, row_tiles in ends:
            band_scores(bank, row_tiles, 0, last_cols)
        quantize_h(b, before, 1)
        band_scores(before_bank, all_rows, b, before_cols)
        store(before_bank, all_rows, before_cols, nc.scalar.copy, nc.sync)
        subtract(b, last)
        quantize_h(b, last, 1)
        for bank, row_tiles in ends:
            band_scores(bank, row_tiles, b, last_cols)
        store(*ends[0], last_cols, nc.vector.tensor_copy, nc.sync)
        store(*ends[1], last_cols, nc.scalar.copy, nc.scalar)
